import numpy as np
import ml_dtypes


def mxq(x, axis, fmt="e4m3"):
    dtype, down = {"e4m3": (ml_dtypes.float8_e4m3fn, 7), "e5m2": (ml_dtypes.float8_e5m2, 14)}[fmt]
    v = np.moveaxis(np.asarray(x, np.float32).astype(ml_dtypes.bfloat16).astype(np.float64), axis, -1)
    blocks = v.reshape(v.shape[:-1] + (-1, 32))
    amax = np.abs(blocks).max(-1, keepdims=True)
    byte = np.maximum(np.where(amax > 0, np.frexp(amax)[1] - 1 + 127, 0) - down, 1)
    scale = np.exp2(byte - 127.0)
    codes = (blocks / scale).astype(np.float32).astype(dtype).astype(np.float64)
    return np.moveaxis((codes * scale).reshape(v.shape), -1, axis)


WIDE = False


def mx_kscale(k):
    if not WIDE:
        return np.ones(k)
    levels = np.array([10, -10, 5, -5, 0])
    if k % 512:
        return np.exp2(np.random.permutation(np.resize(levels, k // 32))).repeat(32)
    a = np.empty((k // 512, 16))
    for p in range(k // 512):
        a[p, :8] = np.random.permutation(np.resize(levels, 8))
        for g in range(8):
            far = levels[np.abs(levels - a[p, g]) >= 10]
            a[p, g + 8] = far[np.random.randint(len(far))]
    return np.exp2(a.ravel()).repeat(32)


BF16 = ml_dtypes.bfloat16


def bf(x):
    return np.asarray(x, np.float32).astype(BF16)


def f64(x):
    return np.asarray(x).astype(np.float64)


E2M1 = np.array([0.0, 0.5, 1.0, 1.5, 2.0, 3.0, 4.0, 6.0, -0.0, -0.5, -1.0, -1.5, -2.0, -3.0, -4.0, -6.0])


def pack_weight(w, fmt):
    k, n = w.shape
    w = f64(bf(w)).reshape(k // 32, 32, n)
    amax = np.abs(w).max(1)
    if fmt == "e4m3":
        byte = np.frexp(amax)[1] - 1 + 127 - 7
    else:
        mant, ex = np.frexp(amax / 6.0)
        byte = np.where(mant > 0.5, ex, ex - 1) + 127
    byte = np.clip(np.where(amax > 0, byte, 1), 1, 254)
    scaled = (w * np.exp2(127.0 - byte)[:, None, :]).reshape(k, n).astype(np.float32)
    by_word = np.ascontiguousarray(scaled.reshape(k // 512, 128, 4, n).transpose(0, 1, 3, 2))
    if fmt == "e4m3":
        words = by_word.astype(ml_dtypes.float8_e4m3fn).view(np.uint8)
    else:
        c = by_word.astype(ml_dtypes.float4_e2m1fn).view(np.uint8) & 0xF
        words = c[..., 0::2] | (c[..., 1::2] << 4)
    return np.ascontiguousarray(words), np.ascontiguousarray(byte.astype(np.uint8).reshape(k // 512, 16, n))


def unpack_weight(words, scales, fmt):
    g, p, n, _ = words.shape
    if fmt == "e4m3":
        vals = np.ascontiguousarray(words).view(ml_dtypes.float8_e4m3fn).astype(np.float64)
    else:
        nib = np.empty((g, p, n, 4), np.uint8)
        nib[..., 0::2] = words & 0xF
        nib[..., 1::2] = words >> 4
        vals = E2M1[nib]
    vals = vals * np.repeat(np.exp2(scales.astype(np.float64) - 127.0), 8, axis=1)[..., None]
    return vals.transpose(0, 1, 3, 2).reshape(g * 512, n)
def pack4(w):
    words, scales = pack_weight(w, "e2m1")
    return words.reshape(words.shape[0], 128, -1), scales


def unpack4(words, scales):
    return unpack_weight(words.reshape(words.shape[0], 128, -1, 2), scales, "e2m1")


B, D, A, V, E, H = 1024, 1024, 128, 8, 4, 512
EPS = 1e-5


def simnorm(l):
    rows, width = l.shape
    grouped = l.reshape(rows, width // V, V)
    e = np.exp(grouped - grouped.max(axis=-1, keepdims=True))
    return (e / e.sum(axis=-1, keepdims=True)).reshape(rows, width)


def plain_layer_norm(q):
    centered = q - np.mean(q, axis=-1, keepdims=True)
    var = np.mean(centered * centered, axis=-1, keepdims=True)
    return centered / np.sqrt(var + EPS)


def mish(x):
    return x * np.tanh(np.log(1.0 + np.exp(x)))


def draw0():
    s, t = mx_kscale(D), mx_kscale(D)
    wq = np.random.standard_normal((E, D, H)) + 0.3 * np.random.standard_normal((E, D, 1))
    z = bf(np.random.standard_normal((B, D)) * s)
    wz_words, wz_scales = pack4(np.random.standard_normal((D, D)) / np.sqrt(D) / s[:, None])
    return {
        "z": z,
        "wz_words": wz_words,
        "wz_scales": wz_scales,
        "a": bf(np.random.standard_normal((B, A)) * 0.7),
        "wa": bf(np.random.standard_normal((A, D)) / np.sqrt(A)),
        "g": bf((1.0 + 0.1 * np.random.standard_normal(D)) * t),
        "wq": bf(wq * 0.016 / np.sqrt(D) / t[:, None]),
    }


def core(z, wz_words, wz_scales, a, wa, g, wq):
    l = (mxq(f64(z), 1, "e4m3") @ unpack4(wz_words, wz_scales)) + f64(a) @ f64(wa)
    s = simnorm(l)
    n = (V * s - 1.0) * f64(g)
    q = mxq(n, 1, "e4m3") @ mxq(f64(wq), 1, "e4m3")
    qn = plain_layer_norm(q)
    return mish(qn)


def e4m3fn_bytes(y):
    return np.clip(np.asarray(y, np.float64), -448.0, 448.0).astype(np.float32).astype(ml_dtypes.float8_e4m3fn).view(np.uint8)


def e4m3fn_values(b):
    return np.asarray(b, np.uint8).view(ml_dtypes.float8_e4m3fn).astype(np.float64)


def setup_inputs():
    d = draw0()
    x0 = np.asarray(d['wq']).astype(np.float64)
    s = (np.max(np.abs(x0), axis=(0, 2), keepdims=True) / 448.0).astype(np.float32)
    out = {}
    for k, v in d.items():
        if k == 'wq':
            out['wq_bytes'] = e4m3fn_bytes(x0 / s.astype(np.float64))
            out['wq_scale'] = s
        else:
            out[k] = v
    return out


def reference(z, wz_words, wz_scales, a, wa, g, wq_bytes, wq_scale):
    return core(z, wz_words, wz_scales, a, wa, g, e4m3fn_values(wq_bytes) * wq_scale.astype(np.float64))

@@ -1,0 +1,570 @@
+from contextlib import ExitStack
+
+import concourse.mybir as mybir
+from concourse.masks import make_identity
+
+B, D, A, V, E, H = 1024, 1024, 128, 8, 4, 512
+EPS = 1e-5
+FLOPS = 2 * B * D * D + 2 * B * A * D + 2 * E * B * D * H
+
+F32 = mybir.dt.float32
+BF16 = mybir.dt.bfloat16
+I32 = mybir.dt.int32
+U32 = mybir.dt.uint32
+U8 = mybir.dt.uint8
+FP8 = mybir.dt.float8_e4m3fn
+FP8X4 = mybir.dt.float8_e4m3fn_x4
+FP4X4 = mybir.dt.float4_e2m1fn_x4
+ALU = mybir.AluOpType
+ACT = mybir.ActivationFunctionType
+AX = mybir.AxisListType
+
+P = 128
+PASSES = D // 512
+TILES = B // P
+PAIR = 2 * P
+GROUPS = D // V
+NORMED = 2
+BANKS = {"vector": 5, "scalar": 3}
+BATCH_ENDS = (3, 7)
+FIRST = 4
+
+
+def tile_tdmpcsimnormdynamicsensemblecritic_w4_kernel(tc, z, wz_words, wz_scales, a, wa, g, wq_bytes, wq_scale, out):
+    nc = tc.nc
+    with ExitStack() as ctx:
+        keep = ctx.enter_context(tc.tile_pool(name="keep", bufs=1))
+        work = ctx.enter_context(tc.tile_pool(name="work", bufs=2))
+        psum = ctx.enter_context(tc.psum_pool(name="psum", bufs=1))
+        ctx.enter_context(tc.manual_schedule())
+
+        def bank(reader, shape, dtype=F32):
+            return psum.tile(shape, dtype, name="bank_" + reader, tag="bank_" + reader, bufs=BANKS[reader])
+
+        ident = keep.tile([P, P], F32, name="ident")
+        ident_bf = keep.tile([P, P], BF16, name="ident_bf")
+        wz_sc = keep.tile([P, PASSES, D], U8, name="wz_sc", align_bytes=64)
+        minus_half = keep.tile([P, E], F32, name="minus_half")
+        nc.gpsimd.memset(wz_sc[:].rearrange("p g n -> p (g n)").bitcast(I32), 0)
+        make_identity(nc, ident[:])
+        make_identity(nc, ident_bf[:])
+        nc.gpsimd.memset(minus_half[:], -0.5)
+
+        z_rows = {}
+        wq_raw = {(e, gp): keep.tile([P, 4, H], U8, name="wq_raw%d_%d" % (e, gp)) for e in range(E) for gp in range(PASSES)}
+        wz_w = keep.tile([P, PASSES, 2 * D], U8, name="wz_w", align_bytes=64)
+        wa_sb = keep.tile([P, D], BF16, name="wa_sb")
+        a_rows = [keep.tile([P, 4, A], BF16, name="a_rows%d" % half) for half in range(2)]
+        wq_sc = keep.tile([P, PASSES, 4], F32, name="wq_sc")
+        g_raw = keep.tile([P, PASSES, 4], BF16, name="g_raw")
+        g8 = keep.tile([P, PASSES, 4], F32, name="g8")
+        a_t = keep.tile([P, B], BF16, name="a_t")
+
+        def load_z(i):
+            z_rows[i] = keep.tile([P, D], BF16, name="z_rows%d" % i)
+            nc.sync.dma_start(out=z_rows[i][:], in_=z[i * P : (i + 1) * P, :])
+
+        def load_wq(e, gp):
+            nc.sync.dma_start(
+                out=wq_raw[e, gp][:].rearrange("p t n -> p (t n)"),
+                in_=wq_bytes[e, 512 * gp : 512 * (gp + 1), :].rearrange("(p t) n -> p (t n)", t=4),
+            )
+
+        def load_a(half):
+            nc.sync.dma_start(out=a_rows[half][:], in_=a[512 * half : 512 * (half + 1), :].rearrange("(i p) k -> p i k", p=P))
+
+        nc.sync.dma_start(out=g_raw[:], in_=g.rearrange("(g p t) -> p g t", p=P, t=4))
+        load_z(0)
+        load_z(1)
+        nc.sync.dma_start(out=wq_sc[:], in_=wq_scale.rearrange("o (g p t) x -> p (o g) (t x)", p=P, t=4))
+        for q in range(4):
+            nc.sync.dma_start(
+                out=wz_sc[32 * q : 32 * q + 4, :, :].bitcast(I32),
+                in_=wz_scales[:, 4 * q : 4 * q + 4, :].rearrange("g r n -> r g n").bitcast(I32),
+            )
+        nc.sync.dma_start(out=wz_w[:].bitcast(I32), in_=wz_words.rearrange("g p n -> p g n").bitcast(I32))
+        load_wq(0, 0)
+        load_a(0)
+        nc.sync.dma_start(out=wa_sb[:], in_=wa[:, :])
+        load_wq(0, 1)
+        load_wq(1, 0)
+        load_z(2)
+        load_z(3)
+        load_wq(1, 1)
+        load_wq(2, 0)
+        load_wq(2, 1)
+        load_wq(3, 0)
+        load_wq(3, 1)
+        load_a(1)
+        for i in range(4, TILES):
+            load_z(i)
+
+        z_grouped, z_codes, z_scales, zw_t = {}, {}, {}, {}
+        logits, shifted, soft, soft_t, n_grouped = {}, {}, {}, {}, {}
+        n_codes = [keep.tile([P, PASSES, P], U32, name="n_codes%d" % i, align_bytes=64) for i in range(TILES)]
+        n_scales = [keep.tile([P, PASSES, P], U8, name="n_scales%d" % i, align_bytes=64) for i in range(TILES)]
+        wq_wide, wq_grouped = {}, {}
+        wq_codes = [keep.tile([P, PASSES, H], U32, name="wq_codes%d" % e, align_bytes=64) for e in range(E)]
+        wq_scales = [keep.tile([P, PASSES, H], U8, name="wq_scales%d" % e, align_bytes=64) for e in range(E)]
+        q_banks, partial, totals = {}, {}, {}
+        moments = [keep.tile([P, E, 2], F32, name="moments%d" % i) for i in range(TILES)]
+        rstd = [keep.tile([P, E], F32, name="rstd%d" % i) for i in range(TILES)]
+        shift = [keep.tile([P, E], F32, name="shift%d" % i) for i in range(TILES)]
+        gate = [keep.tile([P, E, H], F32, name="gate%d" % i) for i in range(TILES)]
+
+        def turn_a(half):
+            turned = bank("scalar", [P, 4, P], BF16)
+            for j in range(4):
+                nc.tensor.transpose(turned[:, j, :], a_rows[half][:, j, :], ident_bf[:])
+            nc.scalar.copy(out=a_t[:, 512 * half : 512 * (half + 1)], in_=turned[:].rearrange("p j r -> p (j r)"))
+
+        def turn_z(i, on_vector=False):
+            pair, hh = divmod(i, 2)
+            if hh == 0:
+                z_grouped[pair] = work.tile([P, PASSES, PAIR, 2], F32, name="z_grouped", align_bytes=64)
+            words = z_rows[i][:].bitcast(F32)
+            turned = bank("vector" if on_vector else "scalar", [P, PASSES, 2, P])
+            for gp in range(PASSES):
+                for u in range(2):
+                    nc.tensor.transpose(turned[:, gp, u, :], words[:, 256 * gp + u : 256 * (gp + 1) : 2], ident[:])
+            dst = z_grouped[pair][:, :, hh * P : (hh + 1) * P, :]
+            src = turned[:].rearrange("p g u r -> p g r u")
+            if on_vector:
+                nc.vector.tensor_copy(out=dst, in_=src)
+            else:
+                nc.scalar.copy(out=dst, in_=src)
+
+        def quantize_z(pair):
+            z_codes[pair] = work.tile([P, PASSES, PAIR], U32, name="z_codes", align_bytes=64)
+            z_scales[pair] = work.tile([P, PASSES, PAIR], U8, name="z_scales", align_bytes=64)
+            nc.vector.quantize_mx(
+                out=z_codes[pair][:].rearrange("p g r -> p (g r)").bitcast(FP8X4),
+                scales=z_scales[pair][:].rearrange("p g r -> p (g r)"),
+                in_=z_grouped[pair][:].rearrange("p g r u -> p (g r u)").bitcast(BF16),
+            )
+
+        def first_product(pair, quarter, on_vector=False):
+            if quarter == 0:
+                zw_t[pair] = work.tile([P, 8, PAIR], F32, name="zw_t")
+            acc = bank("vector" if on_vector else "scalar", [P, 2, PAIR])
+            for cc in range(2):
+                c = 2 * quarter + cc
+                for gp in range(PASSES):
+                    nc.tensor.matmul_mx(
+                        out=acc[:, cc, :],
+                        lhsT=wz_w[:, gp, 2 * P * c : 2 * P * (c + 1)].bitcast(FP4X4),
+                        lhsT_scale=wz_sc[:, gp, P * c : P * (c + 1)],
+                        rhs=z_codes[pair][:, gp, :].bitcast(FP8X4),
+                        rhs_scale=z_scales[pair][:, gp, :],
+                        start=(gp == 0),
+                        stop=(gp == PASSES - 1),
+                    )
+            if on_vector:
+                nc.vector.tensor_copy(out=zw_t[pair][:, 2 * quarter : 2 * quarter + 2, :], in_=acc[:])
+            else:
+                nc.scalar.copy(out=zw_t[pair][:, 2 * quarter : 2 * quarter + 2, :], in_=acc[:])
+
+        def build_logits(i):
+            pair, hh = divmod(i, 2)
+            logits[i] = []
+            for gp in range(PASSES):
+                acc = bank("vector", [P, 512])
+                logits[i].append(acc)
+                nc.tensor.matmul(acc[:], lhsT=a_t[:, i * P : (i + 1) * P], rhs=wa_sb[:, 512 * gp : 512 * (gp + 1)], start=True, stop=False)
+                for c in range(4):
+                    nc.tensor.matmul(
+                        acc[:, c * P : (c + 1) * P],
+                        lhsT=zw_t[pair][:, 4 * gp + c, hh * P : (hh + 1) * P],
+                        rhs=ident[:],
+                        is_transpose=True,
+                        start=False,
+                        stop=(c == 3),
+                    )
+
+        def subtract_max(i):
+            top = work.tile([P, PASSES, 64], F32, name="top")
+            shifted[i] = work.tile([P, 2, PASSES, 256], F32, name="shifted", bufs=3)
+            for gp in range(PASSES):
+                nc.vector.tensor_reduce(out=top[:, gp, :], in_=logits[i][gp][:].rearrange("p (j m) -> p j m", m=V), axis=AX.X, op=ALU.max)
+            for gp in range(PASSES):
+                for h in range(2):
+                    nc.vector.tensor_tensor(
+                        out=shifted[i][:, h, gp, :].rearrange("p (j v w) -> p j v w", v=2, w=2),
+                        in0=logits[i][gp][:].rearrange("p (j v h w) -> p h j v w", v=2, h=2, w=2)[:, h],
+                        in1=top[:, gp, :].unsqueeze(2).unsqueeze(3).to_broadcast([P, 64, 2, 2]),
+                        op=ALU.subtract,
+                    )
+
+        def exponentiate(i):
+            flat = shifted[i][:].rearrange("p h g x -> p (h g x)")
+            nc.scalar.activation(out=flat, in_=flat, func=ACT.Exp)
+
+        def group_sums(i):
+            totals[i] = work.tile([P, GROUPS], F32, name="total")
+            exps = shifted[i][:].rearrange("p h g (j x) -> p (g j) h x", x=4)
+            nc.vector.tensor_reduce(out=totals[i][:], in_=exps, axis=AX.XY, op=ALU.add)
+
+        def normalize(i, engine=None):
+            inverse = work.tile([P, GROUPS], F32, name="inverse")
+            soft[i] = work.tile([P, 2, GROUPS, 4], F32, name="soft")
+            exps = shifted[i][:].rearrange("p h g (j x) -> p h (g j) x", x=4)
+            nc.vector.reciprocal(out=inverse[:], in_=totals[i][:])
+            (engine or nc.gpsimd).tensor_tensor(
+                out=soft[i][:], in0=exps, in1=inverse[:].unsqueeze(1).unsqueeze(3).to_broadcast([P, 2, GROUPS, 4]), op=ALU.mult
+            )
+
+        def turn_soft(i):
+            flat = soft[i][:].rearrange("p h j x -> p h (j x)")
+            soft_t[i] = []
+            for gp in range(PASSES):
+                turned = bank("vector", [P, 4, P])
+                soft_t[i].append(turned)
+                for t in range(4):
+                    h, w = divmod(t, 2)
+                    nc.tensor.transpose(turned[:, t, :], flat[:, h, 256 * gp + w : 256 * (gp + 1) : 2], ident[:])
+
+        def apply_gain(i):
+            n_grouped[i] = work.tile([P, PASSES, P, 4], BF16, name="n_grouped", align_bytes=64)
+            for gp in range(PASSES):
+                nc.vector.scalar_tensor_tensor(
+                    out=n_grouped[i][:, gp, :, :],
+                    in0=soft_t[i][gp][:].rearrange("p t r -> p r t"),
+                    scalar=-1.0 / V,
+                    in1=g8[:, gp, :].unsqueeze(1).to_broadcast([P, P, 4]),
+                    op0=ALU.add,
+                    op1=ALU.mult,
+                )
+
+        def quantize_n(i):
+            nc.vector.quantize_mx(
+                out=n_codes[i][:].rearrange("p g r -> p (g r)").bitcast(FP8X4),
+                scales=n_scales[i][:].rearrange("p g r -> p (g r)"),
+                in_=n_grouped[i][:].rearrange("p g r t -> p (g r t)"),
+            )
+
+        def widen_wq(e, gp, on_vector=False):
+            wq_wide[e, gp] = work.tile([P, 4, H], BF16, name="wq_wide", bufs=3)
+            for t in range(4):
+                src = wq_raw[e, gp][:, t, :].bitcast(FP8)
+                if on_vector:
+                    nc.vector.tensor_scalar(
+                        out=wq_wide[e, gp][:, t, :], in0=src, scalar1=wq_sc[:, gp, t : t + 1], scalar2=None, op0=ALU.mult
+                    )
+                else:
+                    nc.scalar.activation(out=wq_wide[e, gp][:, t, :], in_=src, func=ACT.Copy, scale=wq_sc[:, gp, t : t + 1])
+
+        def group_wq(e, gp, engine):
+            wq_grouped[e, gp] = work.tile([P, H, 4], BF16, name="wq_grouped_" + engine, align_bytes=64, bufs=1)
+            dst = wq_grouped[e, gp][:].rearrange("p (c i) t -> p c t i", i=4)
+            src = wq_wide[e, gp][:].rearrange("p t (c i) -> p c t i", i=4)
+            if engine == "vector":
+                nc.vector.tensor_copy(out=dst, in_=src)
+            elif engine == "scalar":
+                nc.scalar.copy(out=dst, in_=src)
+            else:
+                nc.gpsimd.tensor_scalar(out=dst, in0=src, scalar1=1.0, scalar2=0.0, op0=ALU.mult, op1=ALU.add)
+
+        def quantize_wq(e, gp):
+            nc.vector.quantize_mx(
+                out=wq_codes[e][:, gp, :].bitcast(FP8X4),
+                scales=wq_scales[e][:, gp, :],
+                in_=wq_grouped[e, gp][:].rearrange("p n t -> p (n t)"),
+            )
+
+        def second_product(i, e, reader):
+            acc = bank(reader, [P, H])
+            q_banks[i, e, reader] = acc
+            for gp in range(PASSES):
+                nc.tensor.matmul_mx(
+                    out=acc[:],
+                    lhsT=n_codes[i][:, gp, :].bitcast(FP8X4),
+                    lhsT_scale=n_scales[i][:, gp, :],
+                    rhs=wq_codes[e][:, gp, :].bitcast(FP8X4),
+                    rhs_scale=wq_scales[e][:, gp, :],
+                    start=(gp == 0),
+                    stop=(gp == PASSES - 1),
+                )
+
+        def critics(i, half):
+            for e in (2 * half, 2 * half + 1):
+                second_product(i, e, "vector")
+
+        def statistics(i, half):
+            if half == 0:
+                partial[i] = work.tile([P, E, 6], F32, name="partial")
+            for e in (2 * half, 2 * half + 1):
+                nc.vector.bn_stats(out=partial[i][:, e, :], in_=q_banks[i, e, "vector"][:])
+
+        def norm_factors(i):
+            spread = work.tile([P, E], F32, name="spread")
+            for e in range(E):
+                nc.vector.bn_aggr(out=moments[i][:, e, :], in_=partial[i][:, e, :])
+            flipped = work.tile([P, E], F32, name="flipped")
+            nc.gpsimd.tensor_scalar(out=spread[:], in0=moments[i][:, :, 1], scalar1=EPS, scalar2=1.0, op0=ALU.add, op1=ALU.mult)
+            nc.gpsimd.tensor_tensor(out=rstd[i][:], in0=spread[:], in1=minus_half[:], op=ALU.pow)
+            nc.gpsimd.tensor_scalar(out=flipped[:], in0=moments[i][:, :, 0], scalar1=-1.0, scalar2=0.0, op0=ALU.mult, op1=ALU.add)
+            nc.gpsimd.tensor_tensor(out=shift[i][:], in0=flipped[:], in1=rstd[i][:], op=ALU.mult)
+
+        def gate_exp(i):
+            for e in range(E):
+                second_product(i, e, "scalar")
+                nc.scalar.activation(
+                    out=gate[i][:, e, :], in_=q_banks[i, e, "scalar"][:], func=ACT.Exp, scale=rstd[i][:, e : e + 1], bias=shift[i][:, e : e + 1]
+                )
+
+        def gate_log(i):
+            flat = gate[i][:].rearrange("p e n -> p (e n)")
+            nc.scalar.activation(out=flat, in_=flat, func=ACT.Ln, bias=1.0)
+
+        def gate_tanh(i):
+            flat = gate[i][:].rearrange("p e n -> p (e n)")
+            nc.scalar.activation(out=flat, in_=flat, func=ACT.Tanh)
+
+        def store(i, half):
+            nc.sync.dma_start(
+                out=out[2 * half : 2 * half + 2, i * P : (i + 1) * P, :].rearrange("e p n -> p e n"),
+                in_=gate[i][:, 2 * half : 2 * half + 2, :],
+            )
+
+        def scale_gate(i, half):
+            for e in (2 * half, 2 * half + 1):
+                nc.gpsimd.tensor_scalar(
+                    out=gate[i][:, e, :], in0=gate[i][:, e, :], scalar1=rstd[i][:, e : e + 1], scalar2=0.0, op0=ALU.mult, op1=ALU.add
+                )
+
+        def finish(i, half, scale_here=False):
+            for e in (2 * half, 2 * half + 1):
+                nc.vector.scalar_tensor_tensor(
+                    out=gate[i][:, e, :], in0=q_banks[i, e, "vector"][:], scalar=moments[i][:, e, 0:1], in1=gate[i][:, e, :],
+                    op0=ALU.subtract, op1=ALU.mult,
+                )
+            if scale_here:
+                for e in (2 * half, 2 * half + 1):
+                    nc.vector.tensor_scalar(
+                        out=gate[i][:, e, :], in0=gate[i][:, e, :], scalar1=rstd[i][:, e : e + 1], scalar2=None, op0=ALU.mult
+                    )
+            store(i, half)
+
+        normed = {}
+
+        def keep_normed(i, half):
+            if half == 0:
+                normed[i] = work.tile([P, E, H], F32, name="normed", bufs=NORMED)
+            for e in (2 * half, 2 * half + 1):
+                nc.vector.tensor_scalar(
+                    out=normed[i][:, e, :], in0=q_banks[i, e, "vector"][:], scalar1=rstd[i][:, e : e + 1], scalar2=shift[i][:, e : e + 1],
+                    op0=ALU.mult, op1=ALU.add,
+                )
+
+        def finish_normed(i, half):
+            part = gate[i][:, 2 * half : 2 * half + 2, :]
+            nc.vector.tensor_tensor(out=part, in0=part, in1=normed[i][:, 2 * half : 2 * half + 2, :], op=ALU.mult)
+            store(i, half)
+
+        def gate_tanh_half(i, half):
+            part = gate[i][:, 2 * half : 2 * half + 2, :]
+            nc.scalar.activation(out=part, in_=part, func=ACT.Tanh)
+
+        nc.scalar.activation(out=g8[:], in_=g_raw[:], func=ACT.Copy, scale=float(V))
+        turn_z(0, on_vector=True)
+        turn_z(1, on_vector=True)
+        quantize_z(0)
+        for quarter in range(4):
+            first_product(0, quarter)
+        turn_a(0)
+        widen_wq(0, 0, on_vector=True)
+        group_wq(0, 0, "vector")
+        build_logits(0)
+        build_logits(1)
+        widen_wq(0, 1)
+        group_wq(0, 1, "gpsimd")
+        widen_wq(1, 0)
+        quantize_wq(0, 0)
+        subtract_max(0)
+        exponentiate(0)
+        turn_z(2)
+        turn_z(3)
+        widen_wq(1, 1)
+        subtract_max(1)
+        exponentiate(1)
+        quantize_wq(0, 1)
+        group_wq(1, 0, "gpsimd")
+        widen_wq(2, 0)
+        group_sums(0)
+        normalize(0, nc.vector)
+        turn_soft(0)
+        quantize_wq(1, 0)
+        quantize_z(1)
+        group_wq(1, 1, "gpsimd")
+        for quarter in range(4):
+            first_product(1, quarter)
+        widen_wq(2, 1)
+        group_sums(1)
+        apply_gain(0)
+        normalize(1, nc.vector)
+        build_logits(2)
+        turn_soft(1)
+        quantize_wq(1, 1)
+        quantize_n(0)
+        group_wq(2, 0, "gpsimd")
+        widen_wq(3, 0)
+        group_wq(3, 0, "scalar")
+        critics(0, 0)
+        subtract_max(2)
+        apply_gain(1)
+        quantize_wq(2, 0)
+        group_wq(2, 1, "gpsimd")
+        exponentiate(2)
+        widen_wq(3, 1)
+        build_logits(3)
+        statistics(0, 0)
+        subtract_max(3)
+        quantize_wq(3, 0)
+        group_wq(3, 1, "scalar")
+        quantize_n(1)
+        quantize_wq(2, 1)
+        exponentiate(3)
+        critics(1, 0)
+        group_sums(2)
+        normalize(2)
+        turn_a(1)
+        turn_z(4)
+        turn_z(5)
+        statistics(1, 0)
+        quantize_wq(3, 1)
+        critics(0, 1)
+        critics(1, 1)
+        turn_soft(2)
+        group_sums(3)
+        quantize_z(2)
+        statistics(0, 1)
+        norm_factors(0)
+        for quarter in range(4):
+            first_product(2, quarter)
+        statistics(1, 1)
+        norm_factors(1)
+        apply_gain(2)
+        gate_exp(0)
+        build_logits(4)
+        quantize_n(2)
+        normalize(3)
+        gate_exp(1)
+        critics(2, 0)
+        critics(2, 1)
+        subtract_max(4)
+        turn_soft(3)
+        turn_z(6)
+        turn_z(7)
+        exponentiate(4)
+        gate_log(0)
+        gate_log(1)
+        statistics(2, 0)
+        statistics(2, 1)
+        norm_factors(2)
+        build_logits(5)
+        apply_gain(3)
+        group_sums(4)
+        quantize_z(3)
+        quantize_n(3)
+        normalize(4)
+        critics(3, 0)
+        critics(3, 1)
+        subtract_max(5)
+        for quarter in range(4):
+            first_product(3, quarter)
+        statistics(3, 0)
+        statistics(3, 1)
+        norm_factors(3)
+        turn_soft(4)
+        exponentiate(5)
+        gate_exp(2)
+        gate_tanh(0)
+        apply_gain(4)
+        build_logits(6)
+        group_sums(5)
+        quantize_n(4)
+        normalize(5)
+        critics(4, 0)
+        gate_exp(3)
+        critics(4, 1)
+        subtract_max(6)
+        scale_gate(0, 0)
+        exponentiate(6)
+        gate_tanh(1)
+        statistics(4, 0)
+        statistics(4, 1)
+        norm_factors(4)
+        turn_soft(5)
+        build_logits(7)
+        apply_gain(5)
+        group_sums(6)
+        quantize_n(5)
+        normalize(6)
+        gate_exp(4)
+        critics(5, 0)
+        critics(5, 1)
+        subtract_max(7)
+        scale_gate(0, 1)
+        exponentiate(7)
+        for i in (2, 3, 4):
+            gate_log(i)
+        statistics(5, 0)
+        statistics(5, 1)
+        norm_factors(5)
+        turn_soft(6)
+        apply_gain(6)
+        group_sums(7)
+        quantize_n(6)
+        normalize(7)
+        critics(6, 0)
+        critics(6, 1)
+        scale_gate(1, 0)
+        statistics(6, 0)
+        statistics(6, 1)
+        norm_factors(6)
+        turn_soft(7)
+        gate_exp(5)
+        gate_tanh(2)
+        apply_gain(7)
+        quantize_n(7)
+        critics(7, 0)
+        critics(7, 1)
+        gate_tanh(3)
+        statistics(7, 0)
+        statistics(7, 1)
+        norm_factors(7)
+        critics(0, 0)
+        critics(0, 1)
+        gate_exp(6)
+        gate_tanh(4)
+        scale_gate(1, 1)
+        finish(0, 0)
+        critics(1, 0)
+        finish(0, 1)
+        critics(1, 1)
+        gate_exp(7)
+        finish(1, 0)
+        finish(1, 1)
+        for i in (2, 3, 4):
+            scale_gate(i, 0)
+            scale_gate(i, 1)
+        for i in range(5, TILES):
+            gate_log(i)
+        for i in range(5, TILES):
+            gate_tanh_half(i, 0)
+            gate_tanh_half(i, 1)
+        for i in range(TILES - NORMED, TILES):
+            for half in range(2):
+                critics(i, half)
+                keep_normed(i, half)
+        for i in (2, 3, 4):
+            for half in range(2):
+                critics(i, half)
+                finish(i, half)
+        for i in range(5, TILES - NORMED):
+            for half in range(2):
+                critics(i, half)
+                finish(i, half, scale_here=True)
+        for i in range(TILES - NORMED, TILES):
+            for half in range(2):
+                finish_normed(i, half)

@@ -24,8 +24,8 @@ PASSES = D // 512
 TILES = B // P
 PAIR = 2 * P
 GROUPS = D // V
-NORMED = 2
-BANKS = {"vector": 5, "scalar": 3}
+SCALED = 3
+BANKS = {"vector": 4, "scalar": 4}
 BATCH_ENDS = (3, 7)
 FIRST = 4
 
@@ -47,7 +47,6 @@ def tile_tdmpcsimnormdynamicsensemblecritic_w4_kernel(tc, z, wz_words, wz_scales
         minus_half = keep.tile([P, E], F32, name="minus_half")
         nc.gpsimd.memset(wz_sc[:].rearrange("p g n -> p (g n)").bitcast(I32), 0)
         make_identity(nc, ident[:])
-        make_identity(nc, ident_bf[:])
         nc.gpsimd.memset(minus_half[:], -0.5)
 
         z_rows = {}
@@ -73,21 +72,21 @@ def tile_tdmpcsimnormdynamicsensemblecritic_w4_kernel(tc, z, wz_words, wz_scales
         def load_a(half):
             nc.sync.dma_start(out=a_rows[half][:], in_=a[512 * half : 512 * (half + 1), :].rearrange("(i p) k -> p i k", p=P))
 
-        nc.sync.dma_start(out=g_raw[:], in_=g.rearrange("(g p t) -> p g t", p=P, t=4))
         load_z(0)
         load_z(1)
         nc.sync.dma_start(out=wq_sc[:], in_=wq_scale.rearrange("o (g p t) x -> p (o g) (t x)", p=P, t=4))
+        load_wq(0, 0)
         for q in range(4):
             nc.sync.dma_start(
                 out=wz_sc[32 * q : 32 * q + 4, :, :].bitcast(I32),
                 in_=wz_scales[:, 4 * q : 4 * q + 4, :].rearrange("g r n -> r g n").bitcast(I32),
             )
         nc.sync.dma_start(out=wz_w[:].bitcast(I32), in_=wz_words.rearrange("g p n -> p g n").bitcast(I32))
-        load_wq(0, 0)
+        load_wq(0, 1)
         load_a(0)
         nc.sync.dma_start(out=wa_sb[:], in_=wa[:, :])
-        load_wq(0, 1)
         load_wq(1, 0)
+        nc.sync.dma_start(out=g_raw[:], in_=g.rearrange("(g p t) -> p g t", p=P, t=4))
         load_z(2)
         load_z(3)
         load_wq(1, 1)
@@ -106,11 +105,11 @@ def tile_tdmpcsimnormdynamicsensemblecritic_w4_kernel(tc, z, wz_words, wz_scales
         wq_wide, wq_grouped = {}, {}
         wq_codes = [keep.tile([P, PASSES, H], U32, name="wq_codes%d" % e, align_bytes=64) for e in range(E)]
         wq_scales = [keep.tile([P, PASSES, H], U8, name="wq_scales%d" % e, align_bytes=64) for e in range(E)]
-        q_banks, partial, totals = {}, {}, {}
+        q_banks, partial, totals, tops = {}, {}, {}, {}
         moments = [keep.tile([P, E, 2], F32, name="moments%d" % i) for i in range(TILES)]
         rstd = [keep.tile([P, E], F32, name="rstd%d" % i) for i in range(TILES)]
         shift = [keep.tile([P, E], F32, name="shift%d" % i) for i in range(TILES)]
-        gate = [keep.tile([P, E, H], F32, name="gate%d" % i) for i in range(TILES)]
+        gate = {}
 
         def turn_a(half):
             turned = bank("scalar", [P, 4, P], BF16)
@@ -181,17 +180,21 @@ def tile_tdmpcsimnormdynamicsensemblecritic_w4_kernel(tc, z, wz_words, wz_scales
                         stop=(c == 3),
                     )
 
-        def subtract_max(i):
-            top = work.tile([P, PASSES, 64], F32, name="top")
-            shifted[i] = work.tile([P, 2, PASSES, 256], F32, name="shifted", bufs=3)
+        def group_max(i):
+            tops[i] = work.tile([P, PASSES, 64], F32, name="top")
             for gp in range(PASSES):
-                nc.vector.tensor_reduce(out=top[:, gp, :], in_=logits[i][gp][:].rearrange("p (j m) -> p j m", m=V), axis=AX.X, op=ALU.max)
+                nc.vector.tensor_reduce(
+                    out=tops[i][:, gp, :], in_=logits[i][gp][:].rearrange("p (j m) -> p j m", m=V), axis=AX.X, op=ALU.max
+                )
+
+        def subtract_max(i):
+            shifted[i] = work.tile([P, 2, PASSES, 256], F32, name="shifted", bufs=3)
             for gp in range(PASSES):
                 for h in range(2):
                     nc.vector.tensor_tensor(
                         out=shifted[i][:, h, gp, :].rearrange("p (j v w) -> p j v w", v=2, w=2),
                         in0=logits[i][gp][:].rearrange("p (j v h w) -> p h j v w", v=2, h=2, w=2)[:, h],
-                        in1=top[:, gp, :].unsqueeze(2).unsqueeze(3).to_broadcast([P, 64, 2, 2]),
+                        in1=tops[i][:, gp, :].unsqueeze(2).unsqueeze(3).to_broadcast([P, 64, 2, 2]),
                         op=ALU.subtract,
                     )
 
@@ -254,7 +257,7 @@ def tile_tdmpcsimnormdynamicsensemblecritic_w4_kernel(tc, z, wz_words, wz_scales
                     nc.scalar.activation(out=wq_wide[e, gp][:, t, :], in_=src, func=ACT.Copy, scale=wq_sc[:, gp, t : t + 1])
 
         def group_wq(e, gp, engine):
-            wq_grouped[e, gp] = work.tile([P, H, 4], BF16, name="wq_grouped_" + engine, align_bytes=64, bufs=1)
+            wq_grouped[e, gp] = work.tile([P, H, 4], BF16, name="wq_grouped_" + engine, align_bytes=64, bufs=2 if engine == "vector" else 1)
             dst = wq_grouped[e, gp][:].rearrange("p (c i) t -> p c t i", i=4)
             src = wq_wide[e, gp][:].rearrange("p t (c i) -> p c t i", i=4)
             if engine == "vector":
@@ -297,17 +300,21 @@ def tile_tdmpcsimnormdynamicsensemblecritic_w4_kernel(tc, z, wz_words, wz_scales
 
         def norm_factors(i):
             spread = work.tile([P, E], F32, name="spread")
+            flipped = work.tile([P, E], F32, name="flipped")
             for e in range(E):
                 nc.vector.bn_aggr(out=moments[i][:, e, :], in_=partial[i][:, e, :])
-            flipped = work.tile([P, E], F32, name="flipped")
             nc.gpsimd.tensor_scalar(out=spread[:], in0=moments[i][:, :, 1], scalar1=EPS, scalar2=1.0, op0=ALU.add, op1=ALU.mult)
-            nc.gpsimd.tensor_tensor(out=rstd[i][:], in0=spread[:], in1=minus_half[:], op=ALU.pow)
             nc.gpsimd.tensor_scalar(out=flipped[:], in0=moments[i][:, :, 0], scalar1=-1.0, scalar2=0.0, op0=ALU.mult, op1=ALU.add)
+            nc.gpsimd.tensor_tensor(out=rstd[i][:], in0=spread[:], in1=minus_half[:], op=ALU.pow)
             nc.gpsimd.tensor_tensor(out=shift[i][:], in0=flipped[:], in1=rstd[i][:], op=ALU.mult)
 
-        def gate_exp(i):
+        def gate_feed(i):
             for e in range(E):
                 second_product(i, e, "scalar")
+
+        def gate_exp(i):
+            gate[i] = work.tile([P, E, H], F32, name="gate", tag="row_block", bufs=TILES + 1)
+            for e in range(E):
                 nc.scalar.activation(
                     out=gate[i][:, e, :], in_=q_banks[i, e, "scalar"][:], func=ACT.Exp, scale=rstd[i][:, e : e + 1], bias=shift[i][:, e : e + 1]
                 )
@@ -320,14 +327,14 @@ def tile_tdmpcsimnormdynamicsensemblecritic_w4_kernel(tc, z, wz_words, wz_scales
             flat = gate[i][:].rearrange("p e n -> p (e n)")
             nc.scalar.activation(out=flat, in_=flat, func=ACT.Tanh)
 
-        def store(i, half):
+        def store(i, first, count):
             nc.sync.dma_start(
-                out=out[2 * half : 2 * half + 2, i * P : (i + 1) * P, :].rearrange("e p n -> p e n"),
-                in_=gate[i][:, 2 * half : 2 * half + 2, :],
+                out=out[first : first + count, i * P : (i + 1) * P, :].rearrange("e p n -> p e n"),
+                in_=gate[i][:, first : first + count, :],
             )
 
-        def scale_gate(i, half):
-            for e in (2 * half, 2 * half + 1):
+        def scale_gate(i, first, count=2):
+            for e in range(first, first + count):
                 nc.gpsimd.tensor_scalar(
                     out=gate[i][:, e, :], in0=gate[i][:, e, :], scalar1=rstd[i][:, e : e + 1], scalar2=0.0, op0=ALU.mult, op1=ALU.add
                 )
@@ -343,228 +350,183 @@ def tile_tdmpcsimnormdynamicsensemblecritic_w4_kernel(tc, z, wz_words, wz_scales
                     nc.vector.tensor_scalar(
                         out=gate[i][:, e, :], in0=gate[i][:, e, :], scalar1=rstd[i][:, e : e + 1], scalar2=None, op0=ALU.mult
                     )
-            store(i, half)
+            store(i, 2 * half, 2)
 
         normed = {}
 
-        def keep_normed(i, half):
-            if half == 0:
-                normed[i] = work.tile([P, E, H], F32, name="normed", bufs=NORMED)
-            for e in (2 * half, 2 * half + 1):
+        def keep_normed(i):
+            normed[i] = work.tile([P, E, H], F32, name="normed", tag="row_block", bufs=TILES + 1)
+            for e in range(E):
                 nc.vector.tensor_scalar(
-                    out=normed[i][:, e, :], in0=q_banks[i, e, "vector"][:], scalar1=rstd[i][:, e : e + 1], scalar2=shift[i][:, e : e + 1],
+                    out=normed[i][:, e, :], in0=q_banks[i, e, "scalar"][:], scalar1=rstd[i][:, e : e + 1], scalar2=shift[i][:, e : e + 1],
                     op0=ALU.mult, op1=ALU.add,
                 )
 
-        def finish_normed(i, half):
-            part = gate[i][:, 2 * half : 2 * half + 2, :]
-            nc.vector.tensor_tensor(out=part, in0=part, in1=normed[i][:, 2 * half : 2 * half + 2, :], op=ALU.mult)
-            store(i, half)
+        def finish_normed(i, first, count):
+            part = gate[i][:, first : first + count, :]
+            nc.vector.tensor_tensor(out=part, in0=part, in1=normed[i][:, first : first + count, :], op=ALU.mult)
+            store(i, first, count)
 
-        def gate_tanh_half(i, half):
-            part = gate[i][:, 2 * half : 2 * half + 2, :]
+        def gate_tanh_part(i, first, count):
+            part = gate[i][:, first : first + count, :]
             nc.scalar.activation(out=part, in_=part, func=ACT.Tanh)
 
-        nc.scalar.activation(out=g8[:], in_=g_raw[:], func=ACT.Copy, scale=float(V))
+        nc.scalar.activation(out=ident_bf[:], in_=ident[:], func=ACT.Copy)
+        widen_wq(0, 0)
         turn_z(0, on_vector=True)
         turn_z(1, on_vector=True)
         quantize_z(0)
         for quarter in range(4):
             first_product(0, quarter)
         turn_a(0)
-        widen_wq(0, 0, on_vector=True)
         group_wq(0, 0, "vector")
+        widen_wq(0, 1, on_vector=True)
+        quantize_wq(0, 0)
+        group_wq(0, 1, "vector")
         build_logits(0)
         build_logits(1)
-        widen_wq(0, 1)
-        group_wq(0, 1, "gpsimd")
         widen_wq(1, 0)
-        quantize_wq(0, 0)
+        group_wq(1, 0, "gpsimd")
+        widen_wq(1, 1)
+        quantize_wq(0, 1)
+        group_max(0)
         subtract_max(0)
         exponentiate(0)
+        nc.scalar.activation(out=g8[:], in_=g_raw[:], func=ACT.Copy, scale=float(V))
         turn_z(2)
         turn_z(3)
-        widen_wq(1, 1)
+        widen_wq(2, 0)
+        group_max(1)
         subtract_max(1)
         exponentiate(1)
-        quantize_wq(0, 1)
-        group_wq(1, 0, "gpsimd")
-        widen_wq(2, 0)
+        quantize_wq(1, 0)
+        group_wq(1, 1, "gpsimd")
+        widen_wq(2, 1)
         group_sums(0)
         normalize(0, nc.vector)
         turn_soft(0)
-        quantize_wq(1, 0)
         quantize_z(1)
-        group_wq(1, 1, "gpsimd")
+        quantize_wq(1, 1)
+        group_wq(2, 0, "gpsimd")
+        widen_wq(3, 0)
         for quarter in range(4):
             first_product(1, quarter)
-        widen_wq(2, 1)
         group_sums(1)
         apply_gain(0)
         normalize(1, nc.vector)
         build_logits(2)
         turn_soft(1)
-        quantize_wq(1, 1)
         quantize_n(0)
-        group_wq(2, 0, "gpsimd")
-        widen_wq(3, 0)
-        group_wq(3, 0, "scalar")
-        critics(0, 0)
-        subtract_max(2)
-        apply_gain(1)
         quantize_wq(2, 0)
         group_wq(2, 1, "gpsimd")
-        exponentiate(2)
         widen_wq(3, 1)
-        build_logits(3)
-        statistics(0, 0)
-        subtract_max(3)
-        quantize_wq(3, 0)
         group_wq(3, 1, "scalar")
+        critics(0, 0)
+        group_max(2)
+        subtract_max(2)
+        apply_gain(1)
         quantize_n(1)
         quantize_wq(2, 1)
-        exponentiate(3)
-        critics(1, 0)
-        group_sums(2)
-        normalize(2)
+        group_wq(3, 0, "gpsimd")
+        exponentiate(2)
+        build_logits(3)
         turn_a(1)
-        turn_z(4)
-        turn_z(5)
-        statistics(1, 0)
+        for i in range(4, TILES):
+            turn_z(i)
+        statistics(0, 0)
+        group_max(3)
+        subtract_max(3)
+        exponentiate(3)
         quantize_wq(3, 1)
-        critics(0, 1)
-        critics(1, 1)
-        turn_soft(2)
-        group_sums(3)
+        quantize_wq(3, 0)
         quantize_z(2)
-        statistics(0, 1)
-        norm_factors(0)
+        critics(0, 1)
         for quarter in range(4):
             first_product(2, quarter)
-        statistics(1, 1)
-        norm_factors(1)
-        apply_gain(2)
-        gate_exp(0)
-        build_logits(4)
-        quantize_n(2)
-        normalize(3)
-        gate_exp(1)
-        critics(2, 0)
-        critics(2, 1)
-        subtract_max(4)
-        turn_soft(3)
-        turn_z(6)
-        turn_z(7)
-        exponentiate(4)
-        gate_log(0)
-        gate_log(1)
-        statistics(2, 0)
-        statistics(2, 1)
-        norm_factors(2)
-        build_logits(5)
-        apply_gain(3)
-        group_sums(4)
         quantize_z(3)
-        quantize_n(3)
-        normalize(4)
-        critics(3, 0)
-        critics(3, 1)
-        subtract_max(5)
-        for quarter in range(4):
-            first_product(3, quarter)
-        statistics(3, 0)
-        statistics(3, 1)
-        norm_factors(3)
-        turn_soft(4)
-        exponentiate(5)
-        gate_exp(2)
-        gate_tanh(0)
-        apply_gain(4)
-        build_logits(6)
-        group_sums(5)
-        quantize_n(4)
-        normalize(5)
-        critics(4, 0)
-        gate_exp(3)
-        critics(4, 1)
-        subtract_max(6)
-        scale_gate(0, 0)
-        exponentiate(6)
-        gate_tanh(1)
-        statistics(4, 0)
-        statistics(4, 1)
-        norm_factors(4)
-        turn_soft(5)
-        build_logits(7)
-        apply_gain(5)
-        group_sums(6)
-        quantize_n(5)
-        normalize(6)
-        gate_exp(4)
-        critics(5, 0)
-        critics(5, 1)
-        subtract_max(7)
-        scale_gate(0, 1)
-        exponentiate(7)
-        for i in (2, 3, 4):
-            gate_log(i)
-        statistics(5, 0)
-        statistics(5, 1)
-        norm_factors(5)
-        turn_soft(6)
-        apply_gain(6)
-        group_sums(7)
-        quantize_n(6)
-        normalize(7)
-        critics(6, 0)
-        critics(6, 1)
-        scale_gate(1, 0)
-        statistics(6, 0)
-        statistics(6, 1)
-        norm_factors(6)
-        turn_soft(7)
-        gate_exp(5)
-        gate_tanh(2)
-        apply_gain(7)
+        statistics(0, 1)
+        norm_factors(0)
+        gate_feed(0)
+        to_scale = [(i, e) for i in range(TILES - 2) for e in range(E)]
+        for c in range(2, TILES):
+            group_sums(c)
+            if c > 2:
+                quantize_n(c - 1)
+            normalize(c)
+            critics(c - 1, 0)
+            critics(c - 1, 1)
+            if c % 2 == 0 and 4 <= c:
+                if c + 1 < TILES:
+                    exponentiate(c + 1)
+            gate_exp(c - 2)
+            if c == 2:
+                build_logits(4)
+                for quarter in range(4):
+                    first_product(3, quarter)
+            if c % 2 == 1:
+                gate_log(c - 3)
+                gate_log(c - 2)
+            elif c >= 4:
+                gate_tanh(c - 4)
+                gate_tanh(c - 3)
+            statistics(c - 1, 0)
+            statistics(c - 1, 1)
+            norm_factors(c - 1)
+            if c >= 4:
+                for i, e in to_scale[:SCALED]:
+                    scale_gate(i, e, 1)
+                to_scale = to_scale[SCALED:]
+            if c + 2 < TILES:
+                group_max(c + 2)
+                subtract_max(c + 2)
+                if c % 2 == 0:
+                    exponentiate(c + 2)
+            else:
+                critics(0, c % 2)
+                finish(0, c % 2)
+            turn_soft(c)
+            if c + 3 < TILES:
+                build_logits(c + 3)
+            gate_feed(c - 1)
+            apply_gain(c)
         quantize_n(7)
         critics(7, 0)
         critics(7, 1)
-        gate_tanh(3)
+        for i, e in to_scale[:2]:
+            scale_gate(i, e, 1)
         statistics(7, 0)
+        critics(1, 0)
         statistics(7, 1)
         norm_factors(7)
-        critics(0, 0)
-        critics(0, 1)
-        gate_exp(6)
-        gate_tanh(4)
-        scale_gate(1, 1)
-        finish(0, 0)
-        critics(1, 0)
-        finish(0, 1)
         critics(1, 1)
+        gate_exp(6)
+        keep_normed(6)
+        gate_feed(7)
+        gate_tanh(4)
         gate_exp(7)
+        gate_tanh(5)
+        for i, e in to_scale[2:]:
+            scale_gate(i, e, 1)
+        for i in range(6, TILES):
+            gate_log(i)
+        gate_tanh_part(6, 0, 2)
+        gate_tanh_part(6, 2, 2)
+        gate_tanh_part(7, 0, 2)
+        gate_tanh_part(7, 2, 1)
+        gate_tanh_part(7, 3, 1)
         finish(1, 0)
         finish(1, 1)
-        for i in (2, 3, 4):
-            scale_gate(i, 0)
-            scale_gate(i, 1)
-        for i in range(5, TILES):
-            gate_log(i)
-        for i in range(5, TILES):
-            gate_tanh_half(i, 0)
-            gate_tanh_half(i, 1)
-        for i in range(TILES - NORMED, TILES):
-            for half in range(2):
-                critics(i, half)
-                keep_normed(i, half)
-        for i in (2, 3, 4):
+        critics(2, 0)
+        finish(2, 0)
+        keep_normed(7)
+        critics(2, 1)
+        finish(2, 1)
+        for i in range(3, TILES - 2):
             for half in range(2):
                 critics(i, half)
                 finish(i, half)
-        for i in range(5, TILES - NORMED):
-            for half in range(2):
-                critics(i, half)
-                finish(i, half, scale_here=True)
-        for i in range(TILES - NORMED, TILES):
-            for half in range(2):
-                finish_normed(i, half)
+        finish_normed(6, 0, 2)
+        finish_normed(6, 2, 2)
+        finish_normed(7, 0, 2)
+        finish_normed(7, 2, 1)
+        finish_normed(7, 3, 1)

@@ -24,10 +24,10 @@ PASSES = D // 512
 TILES = B // P
 PAIR = 2 * P
 GROUPS = D // V
+BANKS = 4
+LATE = TILES - 2
 SCALED = 3
-BANKS = {"vector": 4, "scalar": 4}
-BATCH_ENDS = (3, 7)
-FIRST = 4
+SCALED_LAST = 2
 
 
 def tile_tdmpcsimnormdynamicsensemblecritic_w4_kernel(tc, z, wz_words, wz_scales, a, wa, g, wq_bytes, wq_scale, out):
@@ -39,7 +39,7 @@ def tile_tdmpcsimnormdynamicsensemblecritic_w4_kernel(tc, z, wz_words, wz_scales
         ctx.enter_context(tc.manual_schedule())
 
         def bank(reader, shape, dtype=F32):
-            return psum.tile(shape, dtype, name="bank_" + reader, tag="bank_" + reader, bufs=BANKS[reader])
+            return psum.tile(shape, dtype, name="bank_" + reader, tag="bank_" + reader, bufs=BANKS)
 
         ident = keep.tile([P, P], F32, name="ident")
         ident_bf = keep.tile([P, P], BF16, name="ident_bf")
@@ -76,10 +76,10 @@ def tile_tdmpcsimnormdynamicsensemblecritic_w4_kernel(tc, z, wz_words, wz_scales
         load_z(1)
         nc.sync.dma_start(out=wq_sc[:], in_=wq_scale.rearrange("o (g p t) x -> p (o g) (t x)", p=P, t=4))
         load_wq(0, 0)
-        for q in range(4):
+        for quad in range(4):
             nc.sync.dma_start(
-                out=wz_sc[32 * q : 32 * q + 4, :, :].bitcast(I32),
-                in_=wz_scales[:, 4 * q : 4 * q + 4, :].rearrange("g r n -> r g n").bitcast(I32),
+                out=wz_sc[32 * quad : 32 * quad + 4, :, :].bitcast(I32),
+                in_=wz_scales[:, 4 * quad : 4 * quad + 4, :].rearrange("g r n -> r g n").bitcast(I32),
             )
         nc.sync.dma_start(out=wz_w[:].bitcast(I32), in_=wz_words.rearrange("g p n -> p g n").bitcast(I32))
         load_wq(0, 1)
@@ -109,7 +109,7 @@ def tile_tdmpcsimnormdynamicsensemblecritic_w4_kernel(tc, z, wz_words, wz_scales
         moments = [keep.tile([P, E, 2], F32, name="moments%d" % i) for i in range(TILES)]
         rstd = [keep.tile([P, E], F32, name="rstd%d" % i) for i in range(TILES)]
         shift = [keep.tile([P, E], F32, name="shift%d" % i) for i in range(TILES)]
-        gate = {}
+        gate, normed = {}, {}
 
         def turn_a(half):
             turned = bank("scalar", [P, 4, P], BF16)
@@ -142,26 +142,22 @@ def tile_tdmpcsimnormdynamicsensemblecritic_w4_kernel(tc, z, wz_words, wz_scales
                 in_=z_grouped[pair][:].rearrange("p g r u -> p (g r u)").bitcast(BF16),
             )
 
-        def first_product(pair, quarter, on_vector=False):
-            if quarter == 0:
-                zw_t[pair] = work.tile([P, 8, PAIR], F32, name="zw_t")
-            acc = bank("vector" if on_vector else "scalar", [P, 2, PAIR])
-            for cc in range(2):
-                c = 2 * quarter + cc
-                for gp in range(PASSES):
-                    nc.tensor.matmul_mx(
-                        out=acc[:, cc, :],
-                        lhsT=wz_w[:, gp, 2 * P * c : 2 * P * (c + 1)].bitcast(FP4X4),
-                        lhsT_scale=wz_sc[:, gp, P * c : P * (c + 1)],
-                        rhs=z_codes[pair][:, gp, :].bitcast(FP8X4),
-                        rhs_scale=z_scales[pair][:, gp, :],
-                        start=(gp == 0),
-                        stop=(gp == PASSES - 1),
-                    )
-            if on_vector:
-                nc.vector.tensor_copy(out=zw_t[pair][:, 2 * quarter : 2 * quarter + 2, :], in_=acc[:])
-            else:
-                nc.scalar.copy(out=zw_t[pair][:, 2 * quarter : 2 * quarter + 2, :], in_=acc[:])
+        def first_product(pair):
+            zw_t[pair] = work.tile([P, D // P, PAIR], F32, name="zw_t")
+            for c0 in range(0, D // P, 2):
+                acc = bank("scalar", [P, 2, PAIR])
+                for c in (c0, c0 + 1):
+                    for gp in range(PASSES):
+                        nc.tensor.matmul_mx(
+                            out=acc[:, c - c0, :],
+                            lhsT=wz_w[:, gp, 2 * P * c : 2 * P * (c + 1)].bitcast(FP4X4),
+                            lhsT_scale=wz_sc[:, gp, P * c : P * (c + 1)],
+                            rhs=z_codes[pair][:, gp, :].bitcast(FP8X4),
+                            rhs_scale=z_scales[pair][:, gp, :],
+                            start=(gp == 0),
+                            stop=(gp == PASSES - 1),
+                        )
+                nc.scalar.copy(out=zw_t[pair][:, c0 : c0 + 2, :], in_=acc[:])
 
         def build_logits(i):
             pair, hh = divmod(i, 2)
@@ -207,12 +203,12 @@ def tile_tdmpcsimnormdynamicsensemblecritic_w4_kernel(tc, z, wz_words, wz_scales
             exps = shifted[i][:].rearrange("p h g (j x) -> p (g j) h x", x=4)
             nc.vector.tensor_reduce(out=totals[i][:], in_=exps, axis=AX.XY, op=ALU.add)
 
-        def normalize(i, engine=None):
+        def normalize(i, engine):
             inverse = work.tile([P, GROUPS], F32, name="inverse")
             soft[i] = work.tile([P, 2, GROUPS, 4], F32, name="soft")
             exps = shifted[i][:].rearrange("p h g (j x) -> p h (g j) x", x=4)
             nc.vector.reciprocal(out=inverse[:], in_=totals[i][:])
-            (engine or nc.gpsimd).tensor_tensor(
+            engine.tensor_tensor(
                 out=soft[i][:], in0=exps, in1=inverse[:].unsqueeze(1).unsqueeze(3).to_broadcast([P, 2, GROUPS, 4]), op=ALU.mult
             )
 
@@ -257,7 +253,9 @@ def tile_tdmpcsimnormdynamicsensemblecritic_w4_kernel(tc, z, wz_words, wz_scales
                     nc.scalar.activation(out=wq_wide[e, gp][:, t, :], in_=src, func=ACT.Copy, scale=wq_sc[:, gp, t : t + 1])
 
         def group_wq(e, gp, engine):
-            wq_grouped[e, gp] = work.tile([P, H, 4], BF16, name="wq_grouped_" + engine, align_bytes=64, bufs=2 if engine == "vector" else 1)
+            wq_grouped[e, gp] = work.tile(
+                [P, H, 4], BF16, name="wq_grouped_" + engine, align_bytes=64, bufs=2 if engine == "vector" else 1
+            )
             dst = wq_grouped[e, gp][:].rearrange("p (c i) t -> p c t i", i=4)
             src = wq_wide[e, gp][:].rearrange("p t (c i) -> p c t i", i=4)
             if engine == "vector":
@@ -323,9 +321,9 @@ def tile_tdmpcsimnormdynamicsensemblecritic_w4_kernel(tc, z, wz_words, wz_scales
             flat = gate[i][:].rearrange("p e n -> p (e n)")
             nc.scalar.activation(out=flat, in_=flat, func=ACT.Ln, bias=1.0)
 
-        def gate_tanh(i):
-            flat = gate[i][:].rearrange("p e n -> p (e n)")
-            nc.scalar.activation(out=flat, in_=flat, func=ACT.Tanh)
+        def gate_tanh(i, first=0, count=E):
+            part = gate[i][:, first : first + count, :]
+            nc.scalar.activation(out=part, in_=part, func=ACT.Tanh)
 
         def store(i, first, count):
             nc.sync.dma_start(
@@ -333,26 +331,19 @@ def tile_tdmpcsimnormdynamicsensemblecritic_w4_kernel(tc, z, wz_words, wz_scales
                 in_=gate[i][:, first : first + count, :],
             )
 
-        def scale_gate(i, first, count=2):
-            for e in range(first, first + count):
+        def scale_gates(rows):
+            for i, e in rows:
                 nc.gpsimd.tensor_scalar(
                     out=gate[i][:, e, :], in0=gate[i][:, e, :], scalar1=rstd[i][:, e : e + 1], scalar2=0.0, op0=ALU.mult, op1=ALU.add
                 )
 
-        def finish(i, half, scale_here=False):
+        def finish(i, half):
             for e in (2 * half, 2 * half + 1):
                 nc.vector.scalar_tensor_tensor(
                     out=gate[i][:, e, :], in0=q_banks[i, e, "vector"][:], scalar=moments[i][:, e, 0:1], in1=gate[i][:, e, :],
                     op0=ALU.subtract, op1=ALU.mult,
                 )
-            if scale_here:
-                for e in (2 * half, 2 * half + 1):
-                    nc.vector.tensor_scalar(
-                        out=gate[i][:, e, :], in0=gate[i][:, e, :], scalar1=rstd[i][:, e : e + 1], scalar2=None, op0=ALU.mult
-                    )
             store(i, 2 * half, 2)
-
-        normed = {}
 
         def keep_normed(i):
             normed[i] = work.tile([P, E, H], F32, name="normed", tag="row_block", bufs=TILES + 1)
@@ -367,17 +358,12 @@ def tile_tdmpcsimnormdynamicsensemblecritic_w4_kernel(tc, z, wz_words, wz_scales
             nc.vector.tensor_tensor(out=part, in0=part, in1=normed[i][:, first : first + count, :], op=ALU.mult)
             store(i, first, count)
 
-        def gate_tanh_part(i, first, count):
-            part = gate[i][:, first : first + count, :]
-            nc.scalar.activation(out=part, in_=part, func=ACT.Tanh)
-
         nc.scalar.activation(out=ident_bf[:], in_=ident[:], func=ACT.Copy)
         widen_wq(0, 0)
         turn_z(0, on_vector=True)
         turn_z(1, on_vector=True)
         quantize_z(0)
-        for quarter in range(4):
-            first_product(0, quarter)
+        first_product(0)
         turn_a(0)
         group_wq(0, 0, "vector")
         widen_wq(0, 1, on_vector=True)
@@ -385,6 +371,7 @@ def tile_tdmpcsimnormdynamicsensemblecritic_w4_kernel(tc, z, wz_words, wz_scales
         group_wq(0, 1, "vector")
         build_logits(0)
         build_logits(1)
+
         widen_wq(1, 0)
         group_wq(1, 0, "gpsimd")
         widen_wq(1, 1)
@@ -400,6 +387,7 @@ def tile_tdmpcsimnormdynamicsensemblecritic_w4_kernel(tc, z, wz_words, wz_scales
         subtract_max(1)
         exponentiate(1)
         quantize_wq(1, 0)
+
         group_wq(1, 1, "gpsimd")
         widen_wq(2, 1)
         group_sums(0)
@@ -407,10 +395,12 @@ def tile_tdmpcsimnormdynamicsensemblecritic_w4_kernel(tc, z, wz_words, wz_scales
         turn_soft(0)
         quantize_z(1)
         quantize_wq(1, 1)
+
         group_wq(2, 0, "gpsimd")
         widen_wq(3, 0)
-        for quarter in range(4):
-            first_product(1, quarter)
+        first_product(1)
+        turn_z(4)
+        turn_z(5)
         group_sums(1)
         apply_gain(0)
         normalize(1, nc.vector)
@@ -418,6 +408,7 @@ def tile_tdmpcsimnormdynamicsensemblecritic_w4_kernel(tc, z, wz_words, wz_scales
         turn_soft(1)
         quantize_n(0)
         quantize_wq(2, 0)
+
         group_wq(2, 1, "gpsimd")
         widen_wq(3, 1)
         group_wq(3, 1, "scalar")
@@ -426,107 +417,106 @@ def tile_tdmpcsimnormdynamicsensemblecritic_w4_kernel(tc, z, wz_words, wz_scales
         subtract_max(2)
         apply_gain(1)
         quantize_n(1)
+        quantize_z(2)
         quantize_wq(2, 1)
+
         group_wq(3, 0, "gpsimd")
         exponentiate(2)
         build_logits(3)
+        turn_z(6)
+        turn_z(7)
+        first_product(2)
         turn_a(1)
-        for i in range(4, TILES):
-            turn_z(i)
         statistics(0, 0)
         group_max(3)
         subtract_max(3)
         exponentiate(3)
         quantize_wq(3, 1)
         quantize_wq(3, 0)
-        quantize_z(2)
-        critics(0, 1)
-        for quarter in range(4):
-            first_product(2, quarter)
         quantize_z(3)
+        critics(0, 1)
+        first_product(3)
         statistics(0, 1)
         norm_factors(0)
-        gate_feed(0)
-        to_scale = [(i, e) for i in range(TILES - 2) for e in range(E)]
+
+        to_scale = [(i, e) for i in range(LATE) for e in range(E)]
         for c in range(2, TILES):
-            group_sums(c)
-            if c > 2:
+            first_cycle, last_cycle = c == 2, c == TILES - 1
+            if not last_cycle:
+                group_sums(c)
+            if not first_cycle:
                 quantize_n(c - 1)
-            normalize(c)
+            normalize(c, nc.gpsimd)
             critics(c - 1, 0)
             critics(c - 1, 1)
-            if c % 2 == 0 and 4 <= c:
-                if c + 1 < TILES:
-                    exponentiate(c + 1)
+            if c % 2 == 0 and not first_cycle:
+                exponentiate(c + 1)
+            if c + 2 < TILES:
+                build_logits(c + 2)
+            if first_cycle:
+                gate_feed(0)
             gate_exp(c - 2)
-            if c == 2:
-                build_logits(4)
-                for quarter in range(4):
-                    first_product(3, quarter)
             if c % 2 == 1:
                 gate_log(c - 3)
                 gate_log(c - 2)
-            elif c >= 4:
+            elif not first_cycle:
                 gate_tanh(c - 4)
                 gate_tanh(c - 3)
             statistics(c - 1, 0)
             statistics(c - 1, 1)
             norm_factors(c - 1)
-            if c >= 4:
-                for i, e in to_scale[:SCALED]:
-                    scale_gate(i, e, 1)
+            if c >= 4 and c != LATE:
+                scale_gates(to_scale[:SCALED])
                 to_scale = to_scale[SCALED:]
             if c + 2 < TILES:
                 group_max(c + 2)
                 subtract_max(c + 2)
                 if c % 2 == 0:
                     exponentiate(c + 2)
+            elif not last_cycle:
+                group_sums(c + 1)
             else:
-                critics(0, c % 2)
-                finish(0, c % 2)
+                critics(0, 0)
+                finish(0, 0)
             turn_soft(c)
-            if c + 3 < TILES:
-                build_logits(c + 3)
+            if last_cycle:
+                critics(0, 1)
             gate_feed(c - 1)
             apply_gain(c)
-        quantize_n(7)
-        critics(7, 0)
-        critics(7, 1)
-        for i, e in to_scale[:2]:
-            scale_gate(i, e, 1)
-        statistics(7, 0)
+
+        last = TILES - 1
+        quantize_n(last)
+        critics(last, 0)
+        finish(0, 1)
+        critics(last, 1)
+        scale_gates(to_scale[:SCALED_LAST])
+        statistics(last, 0)
         critics(1, 0)
-        statistics(7, 1)
-        norm_factors(7)
+        statistics(last, 1)
+        norm_factors(last)
         critics(1, 1)
-        gate_exp(6)
-        keep_normed(6)
-        gate_feed(7)
-        gate_tanh(4)
-        gate_exp(7)
-        gate_tanh(5)
-        for i, e in to_scale[2:]:
-            scale_gate(i, e, 1)
-        for i in range(6, TILES):
-            gate_log(i)
-        gate_tanh_part(6, 0, 2)
-        gate_tanh_part(6, 2, 2)
-        gate_tanh_part(7, 0, 2)
-        gate_tanh_part(7, 2, 1)
-        gate_tanh_part(7, 3, 1)
+        gate_exp(LATE)
         finish(1, 0)
+        keep_normed(LATE)
+        gate_feed(last)
+        gate_tanh(LATE - 2)
+        gate_exp(last)
+        gate_tanh(LATE - 1)
+        scale_gates(to_scale[SCALED_LAST:])
+        gate_log(LATE)
+        gate_log(last)
+        pieces = [(LATE, 0, 2), (LATE, 2, 2), (last, 0, 2), (last, 2, 1), (last, 3, 1)]
+        for piece in pieces:
+            gate_tanh(*piece)
         finish(1, 1)
         critics(2, 0)
         finish(2, 0)
-        keep_normed(7)
+        keep_normed(last)
         critics(2, 1)
         finish(2, 1)
-        for i in range(3, TILES - 2):
+        for i in range(3, LATE):
             for half in range(2):
                 critics(i, half)
                 finish(i, half)
-        finish_normed(6, 0, 2)
-        finish_normed(6, 2, 2)
-        finish_normed(7, 0, 2)
-        finish_normed(7, 2, 1)
-        finish_normed(7, 3, 1)
+        for piece in pieces:
+            finish_normed(*piece)

@@ -384,11 +384,11 @@ def tile_tdmpcsimnormdynamicsensemblecritic_w4_kernel(tc, z, wz_words, wz_scales
         turn_z(3)
         widen_wq(2, 0)
         group_max(1)
-        subtract_max(1)
-        exponentiate(1)
         quantize_wq(1, 0)
 
         group_wq(1, 1, "gpsimd")
+        subtract_max(1)
+        exponentiate(1)
         widen_wq(2, 1)
         group_sums(0)
         normalize(0, nc.vector)
@@ -465,9 +465,10 @@ def tile_tdmpcsimnormdynamicsensemblecritic_w4_kernel(tc, z, wz_words, wz_scales
             statistics(c - 1, 0)
             statistics(c - 1, 1)
             norm_factors(c - 1)
-            if c >= 4 and c != LATE:
-                scale_gates(to_scale[:SCALED])
-                to_scale = to_scale[SCALED:]
+            if c >= 4:
+                count = 1 if c == LATE else SCALED
+                scale_gates(to_scale[:count])
+                to_scale = to_scale[count:]
             if c + 2 < TILES:
                 group_max(c + 2)
                 subtract_max(c + 2)
@@ -481,7 +482,8 @@ def tile_tdmpcsimnormdynamicsensemblecritic_w4_kernel(tc, z, wz_words, wz_scales
             turn_soft(c)
             if last_cycle:
                 critics(0, 1)
-            gate_feed(c - 1)
+            else:
+                gate_feed(c - 1)
             apply_gain(c)
 
         last = TILES - 1
@@ -489,6 +491,7 @@ def tile_tdmpcsimnormdynamicsensemblecritic_w4_kernel(tc, z, wz_words, wz_scales
         critics(last, 0)
         finish(0, 1)
         critics(last, 1)
+        gate_feed(LATE)
         scale_gates(to_scale[:SCALED_LAST])
         statistics(last, 0)
         critics(1, 0)

from contextlib import ExitStack

import concourse.mybir as mybir
from concourse.masks import make_identity

B, D, A, V, E, H = 1024, 1024, 128, 8, 4, 512
EPS = 1e-5
FLOPS = 2 * B * D * D + 2 * B * A * D + 2 * E * B * D * H

F32 = mybir.dt.float32
BF16 = mybir.dt.bfloat16
I32 = mybir.dt.int32
U32 = mybir.dt.uint32
U8 = mybir.dt.uint8
FP8 = mybir.dt.float8_e4m3fn
FP8X4 = mybir.dt.float8_e4m3fn_x4
FP4X4 = mybir.dt.float4_e2m1fn_x4
ALU = mybir.AluOpType
ACT = mybir.ActivationFunctionType
AX = mybir.AxisListType

P = 128
PASSES = D // 512
TILES = B // P
PAIR = 2 * P
GROUPS = D // V
BANKS = 4
LATE = TILES - 2
SCALED = 3
SCALED_LAST = 2


def tile_tdmpcsimnormdynamicsensemblecritic_w4_kernel(tc, z, wz_words, wz_scales, a, wa, g, wq_bytes, wq_scale, out):
    nc = tc.nc
    with ExitStack() as ctx:
        keep = ctx.enter_context(tc.tile_pool(name="keep", bufs=1))
        work = ctx.enter_context(tc.tile_pool(name="work", bufs=2))
        psum = ctx.enter_context(tc.psum_pool(name="psum", bufs=1))
        ctx.enter_context(tc.manual_schedule())

        def bank(reader, shape, dtype=F32):
            return psum.tile(shape, dtype, name="bank_" + reader, tag="bank_" + reader, bufs=BANKS)

        ident = keep.tile([P, P], F32, name="ident")
        ident_bf = keep.tile([P, P], BF16, name="ident_bf")
        wz_sc = keep.tile([P, PASSES, D], U8, name="wz_sc", align_bytes=64)
        minus_half = keep.tile([P, E], F32, name="minus_half")
        nc.gpsimd.memset(wz_sc[:].rearrange("p g n -> p (g n)").bitcast(I32), 0)
        make_identity(nc, ident[:])
        nc.gpsimd.memset(minus_half[:], -0.5)

        z_rows = {}
        wq_raw = {(e, gp): keep.tile([P, 4, H], U8, name="wq_raw%d_%d" % (e, gp)) for e in range(E) for gp in range(PASSES)}
        wz_w = keep.tile([P, PASSES, 2 * D], U8, name="wz_w", align_bytes=64)
        wa_sb = keep.tile([P, D], BF16, name="wa_sb")
        a_rows = [keep.tile([P, 4, A], BF16, name="a_rows%d" % half) for half in range(2)]
        wq_sc = keep.tile([P, PASSES, 4], F32, name="wq_sc")
        g_raw = keep.tile([P, PASSES, 4], BF16, name="g_raw")
        g8 = keep.tile([P, PASSES, 4], F32, name="g8")
        a_t = keep.tile([P, B], BF16, name="a_t")

        def load_z(i):
            z_rows[i] = keep.tile([P, D], BF16, name="z_rows%d" % i)
            nc.sync.dma_start(out=z_rows[i][:], in_=z[i * P : (i + 1) * P, :])

        def load_wq(e, gp):
            nc.sync.dma_start(
                out=wq_raw[e, gp][:].rearrange("p t n -> p (t n)"),
                in_=wq_bytes[e, 512 * gp : 512 * (gp + 1), :].rearrange("(p t) n -> p (t n)", t=4),
            )

        def load_a(half):
            nc.sync.dma_start(out=a_rows[half][:], in_=a[512 * half : 512 * (half + 1), :].rearrange("(i p) k -> p i k", p=P))

        load_z(0)
        load_z(1)
        nc.sync.dma_start(out=wq_sc[:], in_=wq_scale.rearrange("o (g p t) x -> p (o g) (t x)", p=P, t=4))
        load_wq(0, 0)
        for quad in range(4):
            nc.sync.dma_start(
                out=wz_sc[32 * quad : 32 * quad + 4, :, :].bitcast(I32),
                in_=wz_scales[:, 4 * quad : 4 * quad + 4, :].rearrange("g r n -> r g n").bitcast(I32),
            )
        nc.sync.dma_start(out=wz_w[:].bitcast(I32), in_=wz_words.rearrange("g p n -> p g n").bitcast(I32))
        load_wq(0, 1)
        load_a(0)
        nc.sync.dma_start(out=wa_sb[:], in_=wa[:, :])
        load_wq(1, 0)
        nc.sync.dma_start(out=g_raw[:], in_=g.rearrange("(g p t) -> p g t", p=P, t=4))
        load_z(2)
        load_z(3)
        load_wq(1, 1)
        load_wq(2, 0)
        load_wq(2, 1)
        load_wq(3, 0)
        load_wq(3, 1)
        load_a(1)
        for i in range(4, TILES):
            load_z(i)

        z_grouped, z_codes, z_scales, zw_t = {}, {}, {}, {}
        logits, shifted, soft, soft_t, n_grouped = {}, {}, {}, {}, {}
        n_codes = [keep.tile([P, PASSES, P], U32, name="n_codes%d" % i, align_bytes=64) for i in range(TILES)]
        n_scales = [keep.tile([P, PASSES, P], U8, name="n_scales%d" % i, align_bytes=64) for i in range(TILES)]
        wq_wide, wq_grouped = {}, {}
        wq_codes = [keep.tile([P, PASSES, H], U32, name="wq_codes%d" % e, align_bytes=64) for e in range(E)]
        wq_scales = [keep.tile([P, PASSES, H], U8, name="wq_scales%d" % e, align_bytes=64) for e in range(E)]
        q_banks, partial, totals, tops = {}, {}, {}, {}
        moments = [keep.tile([P, E, 2], F32, name="moments%d" % i) for i in range(TILES)]
        rstd = [keep.tile([P, E], F32, name="rstd%d" % i) for i in range(TILES)]
        shift = [keep.tile([P, E], F32, name="shift%d" % i) for i in range(TILES)]
        gate, normed = {}, {}

        def turn_a(half):
            turned = bank("scalar", [P, 4, P], BF16)
            for j in range(4):
                nc.tensor.transpose(turned[:, j, :], a_rows[half][:, j, :], ident_bf[:])
            nc.scalar.copy(out=a_t[:, 512 * half : 512 * (half + 1)], in_=turned[:].rearrange("p j r -> p (j r)"))

        def turn_z(i, on_vector=False):
            pair, hh = divmod(i, 2)
            if hh == 0:
                z_grouped[pair] = work.tile([P, PASSES, PAIR, 2], F32, name="z_grouped", align_bytes=64)
            words = z_rows[i][:].bitcast(F32)
            turned = bank("vector" if on_vector else "scalar", [P, PASSES, 2, P])
            for gp in range(PASSES):
                for u in range(2):
                    nc.tensor.transpose(turned[:, gp, u, :], words[:, 256 * gp + u : 256 * (gp + 1) : 2], ident[:])
            dst = z_grouped[pair][:, :, hh * P : (hh + 1) * P, :]
            src = turned[:].rearrange("p g u r -> p g r u")
            if on_vector:
                nc.vector.tensor_copy(out=dst, in_=src)
            else:
                nc.scalar.copy(out=dst, in_=src)

        def quantize_z(pair):
            z_codes[pair] = work.tile([P, PASSES, PAIR], U32, name="z_codes", align_bytes=64)
            z_scales[pair] = work.tile([P, PASSES, PAIR], U8, name="z_scales", align_bytes=64)
            nc.vector.quantize_mx(
                out=z_codes[pair][:].rearrange("p g r -> p (g r)").bitcast(FP8X4),
                scales=z_scales[pair][:].rearrange("p g r -> p (g r)"),
                in_=z_grouped[pair][:].rearrange("p g r u -> p (g r u)").bitcast(BF16),
            )

        def first_product(pair):
            zw_t[pair] = work.tile([P, D // P, PAIR], F32, name="zw_t")
            for c0 in range(0, D // P, 2):
                acc = bank("scalar", [P, 2, PAIR])
                for c in (c0, c0 + 1):
                    for gp in range(PASSES):
                        nc.tensor.matmul_mx(
                            out=acc[:, c - c0, :],
                            lhsT=wz_w[:, gp, 2 * P * c : 2 * P * (c + 1)].bitcast(FP4X4),
                            lhsT_scale=wz_sc[:, gp, P * c : P * (c + 1)],
                            rhs=z_codes[pair][:, gp, :].bitcast(FP8X4),
                            rhs_scale=z_scales[pair][:, gp, :],
                            start=(gp == 0),
                            stop=(gp == PASSES - 1),
                        )
                nc.scalar.copy(out=zw_t[pair][:, c0 : c0 + 2, :], in_=acc[:])

        def build_logits(i):
            pair, hh = divmod(i, 2)
            logits[i] = []
            for gp in range(PASSES):
                acc = bank("vector", [P, 512])
                logits[i].append(acc)
                nc.tensor.matmul(acc[:], lhsT=a_t[:, i * P : (i + 1) * P], rhs=wa_sb[:, 512 * gp : 512 * (gp + 1)], start=True, stop=False)
                for c in range(4):
                    nc.tensor.matmul(
                        acc[:, c * P : (c + 1) * P],
                        lhsT=zw_t[pair][:, 4 * gp + c, hh * P : (hh + 1) * P],
                        rhs=ident[:],
                        is_transpose=True,
                        start=False,
                        stop=(c == 3),
                    )

        def group_max(i):
            tops[i] = work.tile([P, PASSES, 64], F32, name="top")
            for gp in range(PASSES):
                nc.vector.tensor_reduce(
                    out=tops[i][:, gp, :], in_=logits[i][gp][:].rearrange("p (j m) -> p j m", m=V), axis=AX.X, op=ALU.max
                )

        def subtract_max(i):
            shifted[i] = work.tile([P, 2, PASSES, 256], F32, name="shifted", bufs=3)
            for gp in range(PASSES):
                for h in range(2):
                    nc.vector.tensor_tensor(
                        out=shifted[i][:, h, gp, :].rearrange("p (j v w) -> p j v w", v=2, w=2),
                        in0=logits[i][gp][:].rearrange("p (j v h w) -> p h j v w", v=2, h=2, w=2)[:, h],
                        in1=tops[i][:, gp, :].unsqueeze(2).unsqueeze(3).to_broadcast([P, 64, 2, 2]),
                        op=ALU.subtract,
                    )

        def exponentiate(i):
            flat = shifted[i][:].rearrange("p h g x -> p (h g x)")
            nc.scalar.activation(out=flat, in_=flat, func=ACT.Exp)

        def group_sums(i):
            totals[i] = work.tile([P, GROUPS], F32, name="total")
            exps = shifted[i][:].rearrange("p h g (j x) -> p (g j) h x", x=4)
            nc.vector.tensor_reduce(out=totals[i][:], in_=exps, axis=AX.XY, op=ALU.add)

        def normalize(i, engine):
            inverse = work.tile([P, GROUPS], F32, name="inverse")
            soft[i] = work.tile([P, 2, GROUPS, 4], F32, name="soft")
            exps = shifted[i][:].rearrange("p h g (j x) -> p h (g j) x", x=4)
            nc.vector.reciprocal(out=inverse[:], in_=totals[i][:])
            engine.tensor_tensor(
                out=soft[i][:], in0=exps, in1=inverse[:].unsqueeze(1).unsqueeze(3).to_broadcast([P, 2, GROUPS, 4]), op=ALU.mult
            )

        def turn_soft(i):
            flat = soft[i][:].rearrange("p h j x -> p h (j x)")
            soft_t[i] = []
            for gp in range(PASSES):
                turned = bank("vector", [P, 4, P])
                soft_t[i].append(turned)
                for t in range(4):
                    h, w = divmod(t, 2)
                    nc.tensor.transpose(turned[:, t, :], flat[:, h, 256 * gp + w : 256 * (gp + 1) : 2], ident[:])

        def apply_gain(i):
            n_grouped[i] = work.tile([P, PASSES, P, 4], BF16, name="n_grouped", align_bytes=64)
            for gp in range(PASSES):
                nc.vector.scalar_tensor_tensor(
                    out=n_grouped[i][:, gp, :, :],
                    in0=soft_t[i][gp][:].rearrange("p t r -> p r t"),
                    scalar=-1.0 / V,
                    in1=g8[:, gp, :].unsqueeze(1).to_broadcast([P, P, 4]),
                    op0=ALU.add,
                    op1=ALU.mult,
                )

        def quantize_n(i):
            nc.vector.quantize_mx(
                out=n_codes[i][:].rearrange("p g r -> p (g r)").bitcast(FP8X4),
                scales=n_scales[i][:].rearrange("p g r -> p (g r)"),
                in_=n_grouped[i][:].rearrange("p g r t -> p (g r t)"),
            )

        def widen_wq(e, gp, on_vector=False):
            wq_wide[e, gp] = work.tile([P, 4, H], BF16, name="wq_wide", bufs=3)
            for t in range(4):
                src = wq_raw[e, gp][:, t, :].bitcast(FP8)
                if on_vector:
                    nc.vector.tensor_scalar(
                        out=wq_wide[e, gp][:, t, :], in0=src, scalar1=wq_sc[:, gp, t : t + 1], scalar2=None, op0=ALU.mult
                    )
                else:
                    nc.scalar.activation(out=wq_wide[e, gp][:, t, :], in_=src, func=ACT.Copy, scale=wq_sc[:, gp, t : t + 1])

        def group_wq(e, gp, engine):
            wq_grouped[e, gp] = work.tile(
                [P, H, 4], BF16, name="wq_grouped_" + engine, align_bytes=64, bufs=2 if engine == "vector" else 1
            )
            dst = wq_grouped[e, gp][:].rearrange("p (c i) t -> p c t i", i=4)
            src = wq_wide[e, gp][:].rearrange("p t (c i) -> p c t i", i=4)
            if engine == "vector":
                nc.vector.tensor_copy(out=dst, in_=src)
            elif engine == "scalar":
                nc.scalar.copy(out=dst, in_=src)
            else:
                nc.gpsimd.tensor_scalar(out=dst, in0=src, scalar1=1.0, scalar2=0.0, op0=ALU.mult, op1=ALU.add)

        def quantize_wq(e, gp):
            nc.vector.quantize_mx(
                out=wq_codes[e][:, gp, :].bitcast(FP8X4),
                scales=wq_scales[e][:, gp, :],
                in_=wq_grouped[e, gp][:].rearrange("p n t -> p (n t)"),
            )

        def second_product(i, e, reader):
            acc = bank(reader, [P, H])
            q_banks[i, e, reader] = acc
            for gp in range(PASSES):
                nc.tensor.matmul_mx(
                    out=acc[:],
                    lhsT=n_codes[i][:, gp, :].bitcast(FP8X4),
                    lhsT_scale=n_scales[i][:, gp, :],
                    rhs=wq_codes[e][:, gp, :].bitcast(FP8X4),
                    rhs_scale=wq_scales[e][:, gp, :],
                    start=(gp == 0),
                    stop=(gp == PASSES - 1),
                )

        def critics(i, half):
            for e in (2 * half, 2 * half + 1):
                second_product(i, e, "vector")

        def statistics(i, half):
            if half == 0:
                partial[i] = work.tile([P, E, 6], F32, name="partial")
            for e in (2 * half, 2 * half + 1):
                nc.vector.bn_stats(out=partial[i][:, e, :], in_=q_banks[i, e, "vector"][:])

        def norm_factors(i):
            spread = work.tile([P, E], F32, name="spread")
            flipped = work.tile([P, E], F32, name="flipped")
            for e in range(E):
                nc.vector.bn_aggr(out=moments[i][:, e, :], in_=partial[i][:, e, :])
            nc.gpsimd.tensor_scalar(out=spread[:], in0=moments[i][:, :, 1], scalar1=EPS, scalar2=1.0, op0=ALU.add, op1=ALU.mult)
            nc.gpsimd.tensor_scalar(out=flipped[:], in0=moments[i][:, :, 0], scalar1=-1.0, scalar2=0.0, op0=ALU.mult, op1=ALU.add)
            nc.gpsimd.tensor_tensor(out=rstd[i][:], in0=spread[:], in1=minus_half[:], op=ALU.pow)
            nc.gpsimd.tensor_tensor(out=shift[i][:], in0=flipped[:], in1=rstd[i][:], op=ALU.mult)

        def gate_feed(i):
            for e in range(E):
                second_product(i, e, "scalar")

        def gate_exp(i):
            gate[i] = work.tile([P, E, H], F32, name="gate", tag="row_block", bufs=TILES + 1)
            for e in range(E):
                nc.scalar.activation(
                    out=gate[i][:, e, :], in_=q_banks[i, e, "scalar"][:], func=ACT.Exp, scale=rstd[i][:, e : e + 1], bias=shift[i][:, e : e + 1]
                )

        def gate_log(i):
            flat = gate[i][:].rearrange("p e n -> p (e n)")
            nc.scalar.activation(out=flat, in_=flat, func=ACT.Ln, bias=1.0)

        def gate_tanh(i, first=0, count=E):
            part = gate[i][:, first : first + count, :]
            nc.scalar.activation(out=part, in_=part, func=ACT.Tanh)

        def store(i, first, count):
            nc.sync.dma_start(
                out=out[first : first + count, i * P : (i + 1) * P, :].rearrange("e p n -> p e n"),
                in_=gate[i][:, first : first + count, :],
            )

        def scale_gates(rows):
            for i, e in rows:
                nc.gpsimd.tensor_scalar(
                    out=gate[i][:, e, :], in0=gate[i][:, e, :], scalar1=rstd[i][:, e : e + 1], scalar2=0.0, op0=ALU.mult, op1=ALU.add
                )

        def finish(i, half):
            for e in (2 * half, 2 * half + 1):
                nc.vector.scalar_tensor_tensor(
                    out=gate[i][:, e, :], in0=q_banks[i, e, "vector"][:], scalar=moments[i][:, e, 0:1], in1=gate[i][:, e, :],
                    op0=ALU.subtract, op1=ALU.mult,
                )
            store(i, 2 * half, 2)

        def keep_normed(i):
            normed[i] = work.tile([P, E, H], F32, name="normed", tag="row_block", bufs=TILES + 1)
            for e in range(E):
                nc.vector.tensor_scalar(
                    out=normed[i][:, e, :], in0=q_banks[i, e, "scalar"][:], scalar1=rstd[i][:, e : e + 1], scalar2=shift[i][:, e : e + 1],
                    op0=ALU.mult, op1=ALU.add,
                )

        def finish_normed(i, first, count):
            part = gate[i][:, first : first + count, :]
            nc.vector.tensor_tensor(out=part, in0=part, in1=normed[i][:, first : first + count, :], op=ALU.mult)
            store(i, first, count)

        nc.scalar.activation(out=ident_bf[:], in_=ident[:], func=ACT.Copy)
        widen_wq(0, 0)
        turn_z(0, on_vector=True)
        turn_z(1, on_vector=True)
        quantize_z(0)
        first_product(0)
        turn_a(0)
        group_wq(0, 0, "vector")
        widen_wq(0, 1, on_vector=True)
        quantize_wq(0, 0)
        group_wq(0, 1, "vector")
        build_logits(0)
        build_logits(1)

        widen_wq(1, 0)
        group_wq(1, 0, "gpsimd")
        widen_wq(1, 1)
        quantize_wq(0, 1)
        group_max(0)
        subtract_max(0)
        exponentiate(0)
        nc.scalar.activation(out=g8[:], in_=g_raw[:], func=ACT.Copy, scale=float(V))
        turn_z(2)
        turn_z(3)
        widen_wq(2, 0)
        group_max(1)
        quantize_wq(1, 0)

        group_wq(1, 1, "gpsimd")
        subtract_max(1)
        exponentiate(1)
        widen_wq(2, 1)
        group_sums(0)
        normalize(0, nc.vector)
        turn_soft(0)
        quantize_z(1)
        quantize_wq(1, 1)

        group_wq(2, 0, "gpsimd")
        widen_wq(3, 0)
        first_product(1)
        turn_z(4)
        turn_z(5)
        group_sums(1)
        apply_gain(0)
        normalize(1, nc.vector)
        build_logits(2)
        turn_soft(1)
        quantize_n(0)
        quantize_wq(2, 0)

        group_wq(2, 1, "gpsimd")
        widen_wq(3, 1)
        group_wq(3, 1, "scalar")
        critics(0, 0)
        group_max(2)
        subtract_max(2)
        apply_gain(1)
        quantize_n(1)
        quantize_z(2)
        quantize_wq(2, 1)

        group_wq(3, 0, "gpsimd")
        exponentiate(2)
        build_logits(3)
        turn_z(6)
        turn_z(7)
        first_product(2)
        turn_a(1)
        statistics(0, 0)
        group_max(3)
        subtract_max(3)
        exponentiate(3)
        quantize_wq(3, 1)
        quantize_wq(3, 0)
        quantize_z(3)
        critics(0, 1)
        first_product(3)
        statistics(0, 1)
        norm_factors(0)

        to_scale = [(i, e) for i in range(LATE) for e in range(E)]
        for c in range(2, TILES):
            first_cycle, last_cycle = c == 2, c == TILES - 1
            if not last_cycle:
                group_sums(c)
            if not first_cycle:
                quantize_n(c - 1)
            normalize(c, nc.gpsimd)
            critics(c - 1, 0)
            critics(c - 1, 1)
            if c % 2 == 0 and not first_cycle:
                exponentiate(c + 1)
            if c + 2 < TILES:
                build_logits(c + 2)
            if first_cycle:
                gate_feed(0)
            gate_exp(c - 2)
            if c % 2 == 1:
                gate_log(c - 3)
                gate_log(c - 2)
            elif not first_cycle:
                gate_tanh(c - 4)
                gate_tanh(c - 3)
            statistics(c - 1, 0)
            statistics(c - 1, 1)
            norm_factors(c - 1)
            if c >= 4:
                count = 1 if c == LATE else SCALED
                scale_gates(to_scale[:count])
                to_scale = to_scale[count:]
            if c + 2 < TILES:
                group_max(c + 2)
                subtract_max(c + 2)
                if c % 2 == 0:
                    exponentiate(c + 2)
            elif not last_cycle:
                group_sums(c + 1)
            else:
                critics(0, 0)
                finish(0, 0)
            turn_soft(c)
            if last_cycle:
                critics(0, 1)
            else:
                gate_feed(c - 1)
            apply_gain(c)

        last = TILES - 1
        quantize_n(last)
        critics(last, 0)
        finish(0, 1)
        critics(last, 1)
        gate_feed(LATE)
        scale_gates(to_scale[:SCALED_LAST])
        statistics(last, 0)
        critics(1, 0)
        statistics(last, 1)
        norm_factors(last)
        critics(1, 1)
        gate_exp(LATE)
        finish(1, 0)
        keep_normed(LATE)
        gate_feed(last)
        gate_tanh(LATE - 2)
        gate_exp(last)
        gate_tanh(LATE - 1)
        scale_gates(to_scale[SCALED_LAST:])
        gate_log(LATE)
        gate_log(last)
        pieces = [(LATE, 0, 2), (LATE, 2, 2), (last, 0, 2), (last, 2, 1), (last, 3, 1)]
        for piece in pieces:
            gate_tanh(*piece)
        finish(1, 1)
        critics(2, 0)
        finish(2, 0)
        keep_normed(last)
        critics(2, 1)
        finish(2, 1)
        for i in range(3, LATE):
            for half in range(2):
                critics(i, half)
                finish(i, half)
        for piece in pieces:
            finish_normed(*piece)
